import numpy as np, ml_dtypes
CORES = [17,25,145,153,273,281,401,409]
N = 8
COUNTS = [[2,1,3,1,8,4,3,1],[1,3,1,2,4,12,1,2],[3,1,2,1,12,4,2,1],[1,2,1,3,4,8,1,3],[2,1,3,1,8,4,3,1],[1,3,1,2,4,12,1,2],[3,1,2,1,12,4,2,1],[1,2,1,3,4,8,1,3]]
XW, YW = 26, 56
def setup_inputs(rng):
    return {"x": rng.standard_normal((N, 128, XW), dtype=np.float32).astype(ml_dtypes.bfloat16)}
def reference(x):
    y = np.full((N, 128, YW), np.nan, x.dtype)
    fill = [0] * N
    for s in range(N):
        o = 0
        for d in range(N):
            c = COUNTS[s][d]
            y[d][:, fill[d]:fill[d] + c] = x[s][:, o:o + c]
            o += c; fill[d] += c
    return {"y": y}

@@ -1,0 +1,121 @@
+import concourse.bass as bass
+
+SCRATCH = {
+    "xb": ("sbuf", [128, 26], "bfloat16"),
+    "hx": ("sbuf", [128, 26], "bfloat16"),
+    "land": ("sbuf", [128, 56], "bfloat16"),
+}
+SEMAPHORES = ["loaded", "own", "stored", "got", "arrived", "sent"]
+
+OFF_CHIP = 0x00FF
+ON_CHIP = 0xFF00
+
+
+def routes(T, topo):
+    cores = list(T.cores)
+    out = []
+    for s, cs in enumerate(cores):
+        hs = topo.host(cs)
+        chip0 = cs % 128 - cs % 8
+        for d, cd in enumerate(cores):
+            if d == s:
+                continue
+            hd = topo.host(cd)
+            same_parity = topo.chip(cs) % 2 == topo.chip(cd) % 2
+            diagonal = (hs ^ hd) == 2
+            if not diagonal and same_parity:
+                via = None
+            elif not diagonal:
+                via = hs * 128 + chip0 + (3 if hd == hs else 6 if hd == (hs ^ 1) else 7)
+            elif same_parity:
+                via = (hs ^ 1) * 128 + chip0 + 4
+            else:
+                via = (3 - hs) * 128 + chip0 + 2
+            out.append((s, d, via))
+    return out
+
+
+def bits(mask):
+    return bin(mask).count("1")
+
+
+def rank_program(g, core, T, topo):
+    cores = list(T.cores)
+    counts = T.tables["COUNTS"]
+    n = len(cores)
+    xo = [[sum(counts[s][:d]) for d in range(n)] for s in range(n)]
+    yo = [[sum(counts[k][d] for k in range(s)) for s in range(n)] for d in range(n)]
+    plan = [r for r in routes(T, topo) if counts[r[0]][r[1]] > 0]
+    sem = T.sem
+
+    def direct_calls(s):
+        ds = [d for (a, d, via) in plan if a == s and via is None]
+        if len(ds) == 2 and counts[s][ds[0]] == counts[s][ds[1]]:
+            return [[(ds[0], 0x000F), (ds[1], 0x00F0)]]
+        return [[(d, OFF_CHIP)] for d in sorted(ds, key=lambda d: -counts[s][d])]
+
+    rank = T.rank_of(core)
+    if rank is None:
+        mine = [(s, d) for (s, d, via) in plan if via == core]
+        if not mine:
+            return
+        s, d = mine[0]
+        c = counts[s][d]
+        rid, pid = topo.addr(cores[d], core)
+        g.wait_ge(sem.got, 8)
+        g.remote_dma(T.land[:, yo[d][s]:yo[d][s] + c], T.hx[:, xo[s][d]:xo[s][d] + c],
+                     sem.arrived, sem.sent, pid, rid, OFF_CHIP)
+        g.wait_ge(sem.sent, 8)
+        return
+
+    s = rank
+    g.dma_start(T.xb[:, :], T.x[:, :]).then_inc(sem.loaded, 16)
+    g.wait_ge(sem.loaded, 16)
+
+    helpers = [via for (a, d, via) in plan if a == s and via is not None]
+    far = sorted([h for h in helpers if h // 8 != core // 8], key=lambda h: h % 8)
+    near = sorted([h for h in helpers if h // 8 == core // 8], key=lambda h: -(h % 8))
+    sent = 0
+    transfers = []
+    for group, mask in ((far, OFF_CHIP), (near, ON_CHIP)):
+        if group:
+            ids = [topo.addr(h, core) for h in group]
+            transfers.append(bass.RemoteDMATransfer(
+                dst_ids=[bass.DstId(rid=r, pnc=p) for (r, p) in ids], dma_engine_mask=mask, remote_sem=sem.got,
+                srcs=[T.xb[:, :]], dsts=[T.hx[:, :] for h in group]))
+            sent += bits(mask)
+    if transfers:
+        g.remote_dma_fused(transfers, local_sem=sem.sent)
+
+    for call in direct_calls(s):
+        trs = []
+        for d, mask in call:
+            c = counts[s][d]
+            rid, pid = topo.addr(cores[d], core)
+            trs.append(bass.RemoteDMATransfer(
+                dst_ids=[bass.DstId(rid=rid, pnc=pid)], dma_engine_mask=mask, remote_sem=sem.arrived,
+                src=T.xb[:, xo[s][d]:xo[s][d] + c], dst=T.land[:, yo[d][s]:yo[d][s] + c]))
+            sent += bits(mask)
+        g.remote_dma_fused(trs, local_sem=sem.sent)
+
+    c = counts[s][s]
+    if c:
+        g.dma_start(T.land[:, yo[s][s]:yo[s][s] + c], T.xb[:, xo[s][s]:xo[s][s] + c]).then_inc(sem.own, 16)
+        g.wait_ge(sem.own, 16)
+
+    due = 0
+    for (a, d, via) in plan:
+        if d == s and via is not None:
+            due += 8
+    for a in range(n):
+        for call in direct_calls(a):
+            for d, mask in call:
+                if d == s:
+                    due += bits(mask)
+    if due:
+        g.wait_ge(sem.arrived, due)
+    total = sum(counts[k][s] for k in range(n))
+    g.dma_start(T.y[:, 0:total], T.land[:, 0:total]).then_inc(sem.stored, 16)
+    if sent:
+        g.wait_ge(sem.sent, sent)
+    g.wait_ge(sem.stored, 16)

@@ -30,7 +30,7 @@ def routes(T, topo):
             elif same_parity:
                 via = (hs ^ 1) * 128 + chip0 + 4
             else:
-                via = (3 - hs) * 128 + chip0 + 2
+                via = (hs ^ 1) * 128 + chip0 + 2
             out.append((s, d, via))
     return out
 
@@ -75,6 +75,9 @@ def rank_program(g, core, T, topo):
     helpers = [via for (a, d, via) in plan if a == s and via is not None]
     far = sorted([h for h in helpers if h // 8 != core // 8], key=lambda h: h % 8)
     near = sorted([h for h in helpers if h // 8 == core // 8], key=lambda h: -(h % 8))
+    need = [d for (a, d, via) in plan if a == s and via is not None]
+    lo = min([xo[s][d] for d in need] + [T.xb.shape[1]])
+    hi = max([xo[s][d] + counts[s][d] for d in need] + [0])
     sent = 0
     transfers = []
     for group, mask in ((far, OFF_CHIP), (near, ON_CHIP)):
@@ -82,7 +85,7 @@ def rank_program(g, core, T, topo):
             ids = [topo.addr(h, core) for h in group]
             transfers.append(bass.RemoteDMATransfer(
                 dst_ids=[bass.DstId(rid=r, pnc=p) for (r, p) in ids], dma_engine_mask=mask, remote_sem=sem.got,
-                srcs=[T.xb[:, :]], dsts=[T.hx[:, :] for h in group]))
+                srcs=[T.xb[:, lo:hi]], dsts=[T.hx[:, lo:hi] for h in group]))
             sent += bits(mask)
     if transfers:
         g.remote_dma_fused(transfers, local_sem=sem.sent)

@@ -13,6 +13,7 @@ ON_CHIP = 0xFF00
 
 def routes(T, topo):
     cores = list(T.cores)
+    counts = T.tables["COUNTS"]
     out = []
     for s, cs in enumerate(cores):
         hs = topo.host(cs)
@@ -32,6 +33,11 @@ def routes(T, topo):
             else:
                 via = (hs ^ 1) * 128 + chip0 + 2
             out.append((s, d, via))
+    for s, cs in enumerate(cores):
+        ds = [d for (a, d, via) in out if a == s and via is None and counts[s][d] > 0]
+        if len(ds) == 2 and counts[s][ds[0]] != counts[s][ds[1]]:
+            wide = max(ds, key=lambda d: counts[s][d])
+            out[out.index((s, wide, None))] = (s, wide, cs - cs % 8)
     return out
 
 
@@ -75,6 +81,8 @@ def rank_program(g, core, T, topo):
     helpers = [via for (a, d, via) in plan if a == s and via is not None]
     far = sorted([h for h in helpers if h // 8 != core // 8], key=lambda h: h % 8)
     near = sorted([h for h in helpers if h // 8 == core // 8], key=lambda h: -(h % 8))
+    while len(near) > len(far) + 1:
+        far.append(near.pop())
     need = [d for (a, d, via) in plan if a == s and via is not None]
     lo = min([xo[s][d] for d in need] + [T.xb.shape[1]])
     hi = max([xo[s][d] + counts[s][d] for d in need] + [0])

import concourse.bass as bass

SCRATCH = {
    "xb": ("sbuf", [128, 26], "bfloat16"),
    "hx": ("sbuf", [128, 26], "bfloat16"),
    "land": ("sbuf", [128, 56], "bfloat16"),
}
SEMAPHORES = ["loaded", "own", "stored", "got", "arrived", "sent"]

OFF_CHIP = 0x00FF
ON_CHIP = 0xFF00


def routes(T, topo):
    cores = list(T.cores)
    counts = T.tables["COUNTS"]
    out = []
    for s, cs in enumerate(cores):
        hs = topo.host(cs)
        chip0 = cs % 128 - cs % 8
        for d, cd in enumerate(cores):
            if d == s:
                continue
            hd = topo.host(cd)
            same_parity = topo.chip(cs) % 2 == topo.chip(cd) % 2
            diagonal = (hs ^ hd) == 2
            if not diagonal and same_parity:
                via = None
            elif not diagonal:
                via = hs * 128 + chip0 + (3 if hd == hs else 6 if hd == (hs ^ 1) else 7)
            elif same_parity:
                via = (hs ^ 1) * 128 + chip0 + 4
            else:
                via = (hs ^ 1) * 128 + chip0 + 2
            out.append((s, d, via))
    for s, cs in enumerate(cores):
        ds = [d for (a, d, via) in out if a == s and via is None and counts[s][d] > 0]
        if len(ds) == 2 and counts[s][ds[0]] != counts[s][ds[1]]:
            wide = max(ds, key=lambda d: counts[s][d])
            out[out.index((s, wide, None))] = (s, wide, cs - cs % 8)
    return out


def bits(mask):
    return bin(mask).count("1")


def rank_program(g, core, T, topo):
    cores = list(T.cores)
    counts = T.tables["COUNTS"]
    n = len(cores)
    xo = [[sum(counts[s][:d]) for d in range(n)] for s in range(n)]
    yo = [[sum(counts[k][d] for k in range(s)) for s in range(n)] for d in range(n)]
    plan = [r for r in routes(T, topo) if counts[r[0]][r[1]] > 0]
    sem = T.sem

    def direct_calls(s):
        ds = [d for (a, d, via) in plan if a == s and via is None]
        if len(ds) == 2 and counts[s][ds[0]] == counts[s][ds[1]]:
            return [[(ds[0], 0x000F), (ds[1], 0x00F0)]]
        return [[(d, OFF_CHIP)] for d in sorted(ds, key=lambda d: -counts[s][d])]

    rank = T.rank_of(core)
    if rank is None:
        mine = [(s, d) for (s, d, via) in plan if via == core]
        if not mine:
            return
        s, d = mine[0]
        c = counts[s][d]
        rid, pid = topo.addr(cores[d], core)
        g.wait_ge(sem.got, 8)
        g.remote_dma(T.land[:, yo[d][s]:yo[d][s] + c], T.hx[:, xo[s][d]:xo[s][d] + c],
                     sem.arrived, sem.sent, pid, rid, OFF_CHIP)
        g.wait_ge(sem.sent, 8)
        return

    s = rank
    g.dma_start(T.xb[:, :], T.x[:, :]).then_inc(sem.loaded, 16)
    g.wait_ge(sem.loaded, 16)

    helpers = [via for (a, d, via) in plan if a == s and via is not None]
    far = sorted([h for h in helpers if h // 8 != core // 8], key=lambda h: h % 8)
    near = sorted([h for h in helpers if h // 8 == core // 8], key=lambda h: -(h % 8))
    while len(near) > len(far) + 1:
        far.append(near.pop())
    need = [d for (a, d, via) in plan if a == s and via is not None]
    lo = min([xo[s][d] for d in need] + [T.xb.shape[1]])
    hi = max([xo[s][d] + counts[s][d] for d in need] + [0])
    sent = 0
    transfers = []
    for group, mask in ((far, OFF_CHIP), (near, ON_CHIP)):
        if group:
            ids = [topo.addr(h, core) for h in group]
            transfers.append(bass.RemoteDMATransfer(
                dst_ids=[bass.DstId(rid=r, pnc=p) for (r, p) in ids], dma_engine_mask=mask, remote_sem=sem.got,
                srcs=[T.xb[:, lo:hi]], dsts=[T.hx[:, lo:hi] for h in group]))
            sent += bits(mask)
    if transfers:
        g.remote_dma_fused(transfers, local_sem=sem.sent)

    for call in direct_calls(s):
        trs = []
        for d, mask in call:
            c = counts[s][d]
            rid, pid = topo.addr(cores[d], core)
            trs.append(bass.RemoteDMATransfer(
                dst_ids=[bass.DstId(rid=rid, pnc=pid)], dma_engine_mask=mask, remote_sem=sem.arrived,
                src=T.xb[:, xo[s][d]:xo[s][d] + c], dst=T.land[:, yo[d][s]:yo[d][s] + c]))
            sent += bits(mask)
        g.remote_dma_fused(trs, local_sem=sem.sent)

    c = counts[s][s]
    if c:
        g.dma_start(T.land[:, yo[s][s]:yo[s][s] + c], T.xb[:, xo[s][s]:xo[s][s] + c]).then_inc(sem.own, 16)
        g.wait_ge(sem.own, 16)

    due = 0
    for (a, d, via) in plan:
        if d == s and via is not None:
            due += 8
    for a in range(n):
        for call in direct_calls(a):
            for d, mask in call:
                if d == s:
                    due += bits(mask)
    if due:
        g.wait_ge(sem.arrived, due)
    total = sum(counts[k][s] for k in range(n))
    g.dma_start(T.y[:, 0:total], T.land[:, 0:total]).then_inc(sem.stored, 16)
    if sent:
        g.wait_ge(sem.sent, sent)
    g.wait_ge(sem.stored, 16)
